import numpy as np
import ml_dtypes


def mxq(x, axis, fmt="e4m3"):
    dtype, down = {"e4m3": (ml_dtypes.float8_e4m3fn, 7), "e5m2": (ml_dtypes.float8_e5m2, 14)}[fmt]
    v = np.moveaxis(np.asarray(x, np.float32).astype(ml_dtypes.bfloat16).astype(np.float64), axis, -1)
    blocks = v.reshape(v.shape[:-1] + (-1, 32))
    amax = np.abs(blocks).max(-1, keepdims=True)
    byte = np.maximum(np.where(amax > 0, np.frexp(amax)[1] - 1 + 127, 0) - down, 1)
    scale = np.exp2(byte - 127.0)
    codes = (blocks / scale).astype(np.float32).astype(dtype).astype(np.float64)
    return np.moveaxis((codes * scale).reshape(v.shape), -1, axis)


WIDE = False


def mx_kscale(k):
    if not WIDE:
        return np.ones(k)
    levels = np.array([10, -10, 5, -5, 0])
    if k % 512:
        return np.exp2(np.random.permutation(np.resize(levels, k // 32))).repeat(32)
    a = np.empty((k // 512, 16))
    for p in range(k // 512):
        a[p, :8] = np.random.permutation(np.resize(levels, 8))
        for g in range(8):
            far = levels[np.abs(levels - a[p, g]) >= 10]
            a[p, g + 8] = far[np.random.randint(len(far))]
    return np.exp2(a.ravel()).repeat(32)


def f64(x):
    return np.asarray(x).astype(np.float64)


def striped(idx):
    return np.tile(idx.reshape(-1, 16).T, (8, 1)).astype(np.uint16)


def unstriped(offs):
    return offs[:16].T.reshape(-1).astype(np.int64)


E2M1 = np.array([0.0, 0.5, 1.0, 1.5, 2.0, 3.0, 4.0, 6.0, -0.0, -0.5, -1.0, -1.5, -2.0, -3.0, -4.0, -6.0])


def pack_weight(w, fmt):
    k, n = w.shape
    w = f64(np.asarray(w, np.float32).astype(ml_dtypes.bfloat16)).reshape(k // 32, 32, n)
    amax = np.abs(w).max(1)
    if fmt == "e4m3":
        byte = np.frexp(amax)[1] - 1 + 127 - 7
    else:
        mant, ex = np.frexp(amax / 6.0)
        byte = np.where(mant > 0.5, ex, ex - 1) + 127
    byte = np.clip(np.where(amax > 0, byte, 1), 1, 254)
    scaled = (w * np.exp2(127.0 - byte)[:, None, :]).reshape(k, n).astype(np.float32)
    by_word = np.ascontiguousarray(scaled.reshape(k // 512, 128, 4, n).transpose(0, 1, 3, 2))
    if fmt == "e4m3":
        words = by_word.astype(ml_dtypes.float8_e4m3fn).view(np.uint8)
    else:
        c = by_word.astype(ml_dtypes.float4_e2m1fn).view(np.uint8) & 0xF
        words = (c[..., 0::2] | (c[..., 1::2] << 4)).reshape(k // 512, 128, 2 * n)
    return np.ascontiguousarray(words), np.ascontiguousarray(byte.astype(np.uint8).reshape(k // 512, 16, n))


def unpack_weight(words, scales, fmt):
    g, _, n = scales.shape
    words = np.ascontiguousarray(words).reshape(g, 128, n, -1)
    if fmt == "e4m3":
        vals = words.view(ml_dtypes.float8_e4m3fn).astype(np.float64)
    else:
        nib = np.empty((g, 128, n, 4), np.uint8)
        nib[..., 0::2] = words & 0xF
        nib[..., 1::2] = words >> 4
        vals = E2M1[nib]
    vals = vals * np.repeat(np.exp2(scales.astype(np.float64) - 127.0), 8, axis=1)[..., None]
    return vals.transpose(0, 1, 3, 2).reshape(g * 512, n)


def gelu(v):
    return 0.5 * v * (1.0 + np.tanh(np.sqrt(2.0 / np.pi) * (v + 0.044715 * v**3)))


K, H, T, S, T2, P = 1024, 1024, 2048, 512, 1024, 512

def setup_inputs():
    n = np.random.standard_normal
    s = mx_kscale(K)[:, None]
    u = mx_kscale(H)[:, None]
    d = {}
    d["tab_words"], d["tab_scales"] = pack_weight(n((K, T)) * s, "e4m3")
    d["offs"] = striped(np.random.permutation(T)[:S])
    d["w1"] = (1.8 * n((K, H)) / K ** 0.5 / s).astype(np.float32)
    d["gain"] = (np.exp(0.3 * n(H)) * u[:, 0]).astype(np.float32)
    d["w2_words"], d["w2_scales"] = pack_weight(n((H, H)) / H ** 0.5 / u * u.T, "e2m1")
    d["wgs"] = np.exp(0.3 * n((128, S))).astype(np.float32)
    d["page0"] = (n((H, T2)) * u).astype(np.float32)
    d["offs2"] = striped(np.random.permutation(T2)[:S])
    d["offs3"] = striped(np.random.permutation(T2)[:P])
    d["lim"] = (n((H, P)) * u).astype(np.float32)
    d["vec"] = (n(H) / H ** 0.5 / u[:, 0] ** 2).astype(np.float32)
    d["slot"] = np.exp(0.4 * n(T2)).astype(np.float32)
    return d

def reference(tab_words, tab_scales, offs, w1, gain, w2_words, w2_scales, wgs, page0, offs2, offs3, lim, vec, slot):
    v = unpack_weight(tab_words, tab_scales, "e4m3")[:, unstriped(offs)]
    w2 = unpack_weight(w2_words, w2_scales, "e2m1")
    act = np.tanh(mxq(f64(w1), 0, "e4m3").T @ v) * f64(gain)[:, None]
    h = np.maximum(w2.T @ mxq(act, 0, "e4m3"), act)
    page = f64(page0).copy()
    page[:, unstriped(offs2)] = np.tile(f64(wgs), (H // 128, 1)) * h
    x = np.maximum(page[:, unstriped(offs3)], f64(lim)) * f64(vec)[:, None]
    e = mxq(page, 0, "e4m3").T @ mxq(x, 0, "e4m3")
    return np.minimum(np.abs(e), f64(slot)[:, None])

@@ -1,0 +1,420 @@
+from contextlib import ExitStack
+
+import concourse.mybir as mybir
+
+K, H, T, S, T2, J = 1024, 1024, 2048, 512, 1024, 512
+FLOPS = 2 * K * H * S + 2 * H * H * S + 2 * H * T2 * J
+
+F32 = mybir.dt.float32
+BF16 = mybir.dt.bfloat16
+I32 = mybir.dt.int32
+U32 = mybir.dt.uint32
+U16 = mybir.dt.uint16
+U8 = mybir.dt.uint8
+FP8X4 = mybir.dt.float8_e4m3fn_x4
+FP4X4 = mybir.dt.float4_e2m1fn_x4
+ALU = mybir.AluOpType
+ACT = mybir.ActivationFunctionType
+
+P = 128
+PACK = 4
+PASS = P * PACK
+PASSES = 2
+SLICES = PASSES * PACK
+QUADS = 4
+
+
+def tile_list_barrier_slot_scores_kernel(
+    tc, tab_words, tab_scales, offs, w1, gain, w2_words, w2_scales, wgs, page0, offs2, offs3, lim, vec, slot, out
+):
+    nc = tc.nc
+    with ExitStack() as ctx:
+        lists = ctx.enter_context(tc.tile_pool(name="lists", bufs=1))
+        keep = ctx.enter_context(tc.tile_pool(name="keep", bufs=1))
+        ring = ctx.enter_context(tc.tile_pool(name="ring", bufs=2))
+        psum = ctx.enter_context(tc.psum_pool(name="psum", bufs=1))
+
+        idx1 = lists.tile([P, S // 16], U16, name="idx1")
+        idx2 = lists.tile([P, S // 16], U16, name="idx2")
+        idx3 = lists.tile([P, J // 16], U16, name="idx3")
+
+        def bank(k):
+            return psum.tile([P, 512], F32, name=f"bank{k}", tag=f"bank{k}")
+
+        HALF = S // 2
+        halves = [slice(0, HALF), slice(HALF, S)]
+        tab_sc = keep.tile([P, T], U8, name="tab_sc", align_bytes=64)
+        w2_sc_raw = keep.tile([P, PASSES, H], U8, name="w2_sc_raw", align_bytes=64)
+        nc.vector.memset(tab_sc[:].bitcast(I32), 0)
+        nc.gpsimd.memset(w2_sc_raw[:].rearrange("p a c -> p (a c)").bitcast(I32), 0)
+        for q in range(QUADS):
+            nc.gpsimd.dma_start(
+                out=w2_sc_raw[32 * q : 32 * q + 4, :, :].bitcast(I32),
+                in_=w2_scales[:, 4 * q : 4 * q + 4, :].rearrange("a r c -> r a c").bitcast(I32),
+            )
+
+        def load_tab_scales(n):
+            a, q = divmod(n, QUADS)
+            nc.sync.dma_start(
+                out=tab_sc[32 * q + 4 * a : 32 * q + 4 * a + 4, :].bitcast(I32),
+                in_=tab_scales[a, 4 * q : 4 * q + 4, :].bitcast(I32),
+            )
+
+        def load_w1(a, c0, width, tag, bufs):
+            raw = keep.tile([P, PACK, width], F32, name=f"w1_raw{a}_{c0}", tag=tag, bufs=bufs, align_bytes=64)
+            nc.sync.dma_start(
+                out=raw[:], in_=w1[PASS * a : PASS * (a + 1), c0 : c0 + width].rearrange("(p j) c -> p j c", j=PACK)
+            )
+            return raw
+
+        def load_tab(a):
+            words = keep.tile([P, T], I32, name=f"tab_w{a}", tag="wide", bufs=2, align_bytes=64)
+            nc.sync.dma_start(out=words[:], in_=tab_words[a].rearrange("p t i -> p (t i)").bitcast(I32))
+            return words
+
+        gain_sb = keep.tile([P, PASSES, PACK], F32, name="gain_sb")
+        w1_raw = {}
+        w1_raw[0, 0] = [load_w1(0, 0, PASS, "w1_raw", 3)]
+        w1_raw[1, 0] = [load_w1(1, 0, PASS, "w1_raw", 3)]
+        for n in range(5):
+            load_tab_scales(n)
+        tab_w = [load_tab(0)]
+        for n in range(5, 8):
+            load_tab_scales(n)
+        nc.sync.dma_start(idx1[:], offs)
+        tab_w.append(load_tab(1))
+        nc.sync.dma_start(out=gain_sb[:], in_=gain.rearrange("(b p t) -> p b t", b=PASSES, t=PACK))
+        w1_raw[0, 1] = [load_w1(0, PASS, PASS, "w1_raw", 3)]
+        w1_raw[1, 1] = [load_w1(1, PASS + PASS // 2 * n, PASS // 2, "w1_last", 2) for n in range(2)]
+
+        w2_raw = [keep.tile([P, PASSES, H], U8, name=f"w2_raw{b}", align_bytes=64) for b in range(PASSES)]
+        wgs_sb = keep.tile([P, PACK, S], F32, name="wgs_sb")
+        wgs_rows = wgs.rearrange("(q t) j -> q t j", t=PACK)
+        page = [keep.tile([P, T2], F32, name=f"page{k}", tag=f"page{k}") for k in range(SLICES)]
+        lim_sb = [keep.tile([P, J], F32, name=f"lim{k}") for k in range(SLICES)]
+        vec_sb = keep.tile([P, PASSES, PACK], F32, name="vec_sb")
+        slot_sb = keep.tile([P, T2 // P], F32, name="slot_sb")
+
+        def load_w2(b):
+            nc.sync.dma_start(
+                out=w2_raw[b][:].bitcast(I32),
+                in_=w2_words[:, :, H * b : H * (b + 1)].rearrange("a p c -> p a c").bitcast(I32),
+            )
+
+        def load_wgs(cols):
+            for q in range(QUADS):
+                nc.sync.dma_start(out=wgs_sb[32 * q : 32 * (q + 1), :, cols], in_=wgs_rows[:, :, cols])
+
+        def load_rows(dst, src, k):
+            b, t = divmod(k, PACK)
+            rows = src[PASS * b : PASS * (b + 1), :].rearrange("(p t) m -> p t m", t=PACK)
+            nc.sync.dma_start(out=dst[k][:], in_=rows[:, t, :])
+
+        load_w2(0)
+        nc.sync.dma_start(idx2[:], offs2)
+        load_wgs(halves[0])
+        load_rows(page, page0, 0)
+        load_rows(page, page0, 1)
+        load_w2(1)
+        load_wgs(halves[1])
+        load_rows(page, page0, 2)
+        nc.sync.dma_start(idx3[:], offs3)
+        nc.sync.dma_start(out=vec_sb[:], in_=vec.rearrange("(b p t) -> p b t", b=PASSES, t=PACK))
+        load_rows(lim_sb, lim, 0)
+        load_rows(lim_sb, lim, 1)
+        for k in range(3, SLICES):
+            load_rows(page, page0, k)
+            load_rows(lim_sb, lim, k - 1)
+        load_rows(lim_sb, lim, SLICES - 1)
+        with nc.allow_non_contiguous_dma(reason="one float32 for each partition and output tile"):
+            nc.sync.dma_start(out=slot_sb[:], in_=slot.rearrange("(i p) -> p i", p=P))
+
+        w2_codes = [keep.tile([P, PASSES, H], U8, name=f"w2_codes{b}", align_bytes=64) for b in range(PASSES)]
+        w2_sc = keep.tile([P, PASSES, H], U8, name="w2_sc", align_bytes=64)
+        nc.vector.tensor_copy(
+            out=w2_sc[:].rearrange("p a (b t q) -> p (a b) t q", t=PACK, q=P),
+            in_=w2_sc_raw[:].rearrange("p a (b q t) -> p (a b) t q", t=PACK, q=P),
+        )
+
+        def deal_w2(b):
+            nc.vector.tensor_copy(
+                out=w2_codes[b][:].rearrange("p a c -> p (a c)").bitcast(U16).rearrange("p (a t q) -> p a t q", t=PACK, q=P),
+                in_=w2_raw[b][:].rearrange("p a c -> p (a c)").bitcast(U16).rearrange("p (a q t) -> p a t q", t=PACK, q=P),
+            )
+
+        w1_codes = {}
+        w1_sc = {}
+
+        def prepare_w1(a, b, on_scalar, quant_parts):
+            grouped = ring.tile([P, PACK, P, PACK], BF16, name="w1_bf", align_bytes=64)
+            dst = grouped[:].rearrange("p t m j -> p m t j")
+            share = P // len(w1_raw[a, b])
+            for n, raw in enumerate(w1_raw[a, b]):
+                src = raw[:].rearrange("p j (m t) -> p m t j", t=PACK)
+                if on_scalar:
+                    nc.scalar.copy(out=dst[:, share * n : share * (n + 1), :, :], in_=src)
+                else:
+                    nc.vector.tensor_copy(out=dst[:, share * n : share * (n + 1), :, :], in_=src)
+            codes = keep.tile([P, PASS], U32, name=f"w1_codes{a}{b}", align_bytes=64)
+            scales = keep.tile([P, PASS], U8, name=f"w1_sc{a}{b}", align_bytes=64)
+            flat = grouped[:].rearrange("p t m j -> p (t m j)")
+            width = PASS // quant_parts
+            for n in range(quant_parts):
+                cols = slice(width * n, width * (n + 1))
+                nc.vector.quantize_mx(
+                    out=codes[:, cols].bitcast(FP8X4),
+                    scales=scales[:, cols],
+                    in_=flat[:, PACK * width * n : PACK * width * (n + 1)],
+                )
+            w1_codes[a, b] = codes
+            w1_sc[a, b] = scales
+
+        v_sc = keep.tile([P, S], U8, name="v_sc", align_bytes=64)
+        v_w = [keep.tile([P, S], U32, name=f"v_w{a}", align_bytes=64) for a in range(PASSES)]
+
+        def stage1(dst, a, b, t, cols, start, stop):
+            m_cols = slice(P * t, P * (t + 1))
+            nc.tensor.matmul_mx(
+                out=dst,
+                lhsT=w1_codes[a, b][:, m_cols].bitcast(FP8X4),
+                lhsT_scale=w1_sc[a, b][:, m_cols],
+                rhs=v_w[a][:, cols].bitcast(FP8X4),
+                rhs_scale=v_sc[4 * a : P, cols],
+                start=start,
+                stop=stop,
+            )
+
+        th = [keep.tile([P, PACK, S], F32, name=f"th{b}") for b in range(PASSES)]
+        act_codes = [keep.tile([P, S], U32, name=f"act_codes{b}", align_bytes=64) for b in range(PASSES)]
+        act_sc = [keep.tile([P, S], U8, name=f"act_sc{b}", align_bytes=64) for b in range(PASSES)]
+        planes = {
+            (b, u): keep.tile([P, PACK, HALF], BF16, name=f"act_planes{b}{u}", align_bytes=64)
+            for b in range(PASSES)
+            for u in range(2)
+        }
+
+        def scale_act(b, t, u):
+            nc.scalar.activation(
+                out=planes[b, u][:, t, :], in_=th[b][:, t, halves[u]], func=ACT.Copy, scale=gain_sb[:, b, t : t + 1]
+            )
+
+        def weave(engine, woven, src):
+            dst_view = woven.rearrange("p (c i) t -> p c t i", i=4)
+            src_view = src.rearrange("p t (c i) -> p c t i", i=4)
+            if engine == "scalar":
+                nc.scalar.copy(out=dst_view, in_=src_view)
+            else:
+                nc.vector.tensor_copy(out=dst_view, in_=src_view)
+
+        woven_act = {}
+
+        def weave_act(b, u, engine):
+            woven_act[b, u] = keep.tile([P, HALF, PACK], BF16, name=f"act_woven{b}{u}", align_bytes=64)
+            weave(engine, woven_act[b, u][:], planes[b, u][:])
+
+        def quant_act(b, u):
+            nc.vector.quantize_mx(
+                out=act_codes[b][:, halves[u]].bitcast(FP8X4),
+                scales=act_sc[b][:, halves[u]],
+                in_=woven_act[b, u][:].rearrange("p j t -> p (j t)"),
+            )
+
+        everything = slice(0, S)
+        prepare_w1(0, 0, True, 1)
+        prepare_w1(1, 0, True, 1)
+        nc.vector.tensor_copy(v_sc[:], tab_sc[:].indirect(idx1[:]))
+        y_low = [bank(PACK + t) for t in range(PACK)]
+        for a in range(PASSES):
+            nc.vector.tensor_copy(v_w[a][:], tab_w[a][:].bitcast(U32).indirect(idx1[:]))
+            for t in range(PACK):
+                stage1(y_low[t][:], a, 0, t, everything, a == 0, a == PASSES - 1)
+        for t in range(PACK):
+            nc.scalar.activation(out=th[0][:, t, :], in_=y_low[t][:], func=ACT.Tanh)
+            scale_act(0, t, 0)
+        y_high = [bank(n) for n in range(PACK)]
+        for a in range(PASSES):
+            prepare_w1(a, 1, False, 1 + a)
+            for u in range(2):
+                for t in range(PACK):
+                    dst = y_high[2 * u + t // 2][:, HALF * (t % 2) : HALF * (t % 2 + 1)]
+                    stage1(dst, a, 1, t, halves[u], a == 0 and t % 2 == 0, a == PASSES - 1 and t % 2 == 1)
+        weave_act(0, 0, "vector")
+        quant_act(0, 0)
+        deal_w2(0)
+        for u in range(2):
+            for pair in range(2):
+                nc.scalar.activation(
+                    out=th[1][:, 2 * pair : 2 * pair + 2, halves[u]],
+                    in_=y_high[2 * u + pair][:].rearrange("p (t j) -> p t j", t=2),
+                    func=ACT.Tanh,
+                )
+                for t in range(2 * pair, 2 * pair + 2):
+                    scale_act(1, t, u)
+            if u == 0:
+                weave_act(1, 0, "vector")
+                quant_act(1, 0)
+        weave_act(1, 1, "scalar")
+        for t in range(PACK):
+            scale_act(0, t, 1)
+        weave_act(0, 1, "scalar")
+
+        y2 = {}
+
+        def stage2(k, cols):
+            b, t = divmod(k, PACK)
+            if k not in y2:
+                y2[k] = bank((k + PACK) % SLICES)
+            width = S if cols == everything else P
+            starts = list(range(cols.start, cols.stop, width))
+            for a in range(PASSES):
+                for c0 in starts:
+                    nc.tensor.matmul_mx(
+                        out=y2[k][:, c0 : c0 + width],
+                        lhsT=w2_codes[b][:, a, 2 * P * t : 2 * P * (t + 1)].bitcast(FP4X4),
+                        lhsT_scale=w2_sc[:, a, P * k : P * (k + 1)],
+                        rhs=act_codes[a][:, c0 : c0 + width].bitcast(FP8X4),
+                        rhs_scale=act_sc[a][:, c0 : c0 + width],
+                        start=(a == 0 and c0 == starts[0]),
+                        stop=(a == PASSES - 1 and c0 == starts[-1]),
+                    )
+
+        page_planes = keep.tile([P, PACK, T2], BF16, name="page_planes", align_bytes=64)
+        x_planes = keep.tile([P, PACK, J], BF16, name="x_planes", align_bytes=64)
+        page_bf = [
+            keep.tile([P, T2, PACK], BF16, name=f"page_bf{b}", tag="wide", bufs=2, align_bytes=64) for b in range(PASSES)
+        ]
+        x_bf = [keep.tile([P, J, PACK], BF16, name=f"x_bf{b}", tag=f"x_bf{b}", align_bytes=64) for b in range(PASSES)]
+        page_codes = [keep.tile([P, T2], U32, name=f"page_codes{b}", align_bytes=64) for b in range(PASSES)]
+        page_sc = [keep.tile([P, T2], U8, name=f"page_sc{b}", align_bytes=64) for b in range(PASSES)]
+        x_codes = [keep.tile([P, J], U32, name=f"x_codes{b}", align_bytes=64) for b in range(PASSES)]
+        x_sc = [keep.tile([P, J], U8, name=f"x_sc{b}", align_bytes=64) for b in range(PASSES)]
+        e = {}
+        h = {}
+        picked = {}
+        top = {}
+        last = SLICES - 1
+
+        def meet(k, cols, dst=None):
+            b, t = divmod(k, PACK)
+            if dst is None:
+                fresh = ring.tile([P, S], F32, name="h", bufs=3)
+                dst = fresh[:]
+            h[k, cols.start] = dst[:, cols]
+            nc.vector.scalar_tensor_tensor(
+                dst[:, cols], th[b][:, t, cols], gain_sb[:, b, t : t + 1], y2[k][:, cols], ALU.mult, ALU.max
+            )
+
+        def put(k, cols):
+            places = idx2[:, cols.start // 16 : cols.stop // 16]
+            nc.vector.tensor_tensor(page[k][:].indirect(places), h[k, cols.start], wgs_sb[:, k % PACK, cols], ALU.mult)
+
+        def round_page(k, cols):
+            b, t = divmod(k, PACK)
+            dst = page_planes[:, t, cols] if b == 0 else page_bf[b][:, cols, t]
+            nc.scalar.copy(out=dst, in_=page[k][:, cols])
+
+        def pick(k, dst=None):
+            if dst is None:
+                fresh = ring.tile([P, J], F32, name="picked")
+                dst = fresh[:]
+            picked[k] = dst
+            nc.vector.tensor_copy(dst, page[k][:].indirect(idx3[:]))
+
+        def limit(k):
+            b, t = divmod(k, PACK)
+            top[k] = top[k - 1] if k == last else ring.tile([P, J], F32, name="top", bufs=4)
+            nc.vector.tensor_tensor(top[k][:], picked[k], lim_sb[k][:], ALU.max)
+            factor = vec_sb[:, b, t : t + 1]
+            if k == last:
+                nc.vector.tensor_scalar(x_bf[b][:, :, t], top[k][:], factor, None, ALU.mult)
+            else:
+                dst = x_planes[:, t, :] if b == 0 else x_bf[b][:, :, t]
+                nc.scalar.activation(out=dst, in_=top[k][:], func=ACT.Copy, scale=factor)
+
+        def quant_page(b, cols):
+            nc.vector.quantize_mx(
+                out=page_codes[b][:, cols].bitcast(FP8X4),
+                scales=page_sc[b][:, cols],
+                in_=page_bf[b][:, cols, :].rearrange("p m t -> p (m t)"),
+            )
+
+        def quant_x(b):
+            nc.vector.quantize_mx(
+                out=x_codes[b][:].bitcast(FP8X4), scales=x_sc[b][:], in_=x_bf[b][:].rearrange("p j t -> p (j t)")
+            )
+
+        def stage3(i, b):
+            if b == 0:
+                e[i] = bank((i + PACK) % SLICES)
+            cols = slice(P * i, P * (i + 1))
+            nc.tensor.matmul_mx(
+                out=e[i][:],
+                lhsT=page_codes[b][:, cols].bitcast(FP8X4),
+                lhsT_scale=page_sc[b][:, cols],
+                rhs=x_codes[b][:].bitcast(FP8X4),
+                rhs_scale=x_sc[b][:],
+                start=(b == 0),
+                stop=(b == PASSES - 1),
+            )
+
+        whole = slice(0, T2)
+        early = 3
+        for k in range(early):
+            stage2(k, halves[0])
+        meet(0, halves[0])
+        meet(1, halves[0])
+        put(0, halves[0])
+        meet(2, halves[0])
+        put(1, halves[0])
+        quant_act(1, 1)
+        quant_act(0, 1)
+        deal_w2(1)
+        for k in range(early):
+            stage2(k, halves[1])
+        for k in range(early, SLICES):
+            stage2(k, everything)
+        put(2, halves[0])
+        units = [(k, halves[1] if k < early else everything) for k in range(SLICES)]
+        meet(*units[0])
+        for k in range(last):
+            if k + 1 < last:
+                meet(*units[k + 1])
+            if k > 0:
+                pick(k - 1)
+            put(*units[k])
+            round_page(k, whole)
+            if k == PACK - 1:
+                weave("scalar", page_bf[0][:], page_planes[:])
+            if k > 0:
+                limit(k - 1)
+            if k == PACK:
+                weave("scalar", x_bf[0][:], x_planes[:])
+        quant_page(0, whole)
+        quant_x(0)
+        late = keep.tile([P, 2, S], F32, name="late", tag="x_bf0", align_bytes=64)
+        for i in range(last):
+            stage3(i, 0)
+        pick(last - 1, late[:, 0, :])
+        meet(last, everything, late[:, 1, :])
+        stage3(last, 0)
+        limit(last - 1)
+        put(last, everything)
+        chunk = 256
+        for c in range(T2 // chunk):
+            round_page(last, slice(chunk * c, chunk * (c + 1)))
+        pick(last)
+        quant_page(1, slice(0, chunk))
+        limit(last)
+        quant_page(1, slice(chunk, 2 * chunk))
+        quant_x(1)
+        for c in range(T2 // chunk):
+            if c >= 2:
+                quant_page(1, slice(chunk * c, chunk * (c + 1)))
+            for i in range(2 * c, 2 * c + 2):
+                stage3(i, 1)
+
+        for i in range(T2 // P):
+            staged = keep.tile([P, 2, J], F32, name=f"staged{i}", tag=f"page{i}")
+            nc.scalar.activation(out=staged[:, 0, :], in_=e[i][:], func=ACT.Abs)
+            nc.vector.tensor_scalar(staged[:, 1, :], staged[:, 0, :], slot_sb[:, i : i + 1], None, ALU.min)
+            nc.sync.dma_start(out=out[P * i : P * (i + 1), :], in_=staged[:, 1, :])

@@ -45,20 +45,8 @@ def tile_list_barrier_slot_scores_kernel(
         halves = [slice(0, HALF), slice(HALF, S)]
         tab_sc = keep.tile([P, T], U8, name="tab_sc", align_bytes=64)
         w2_sc_raw = keep.tile([P, PASSES, H], U8, name="w2_sc_raw", align_bytes=64)
-        nc.vector.memset(tab_sc[:].bitcast(I32), 0)
-        nc.gpsimd.memset(w2_sc_raw[:].rearrange("p a c -> p (a c)").bitcast(I32), 0)
-        for q in range(QUADS):
-            nc.gpsimd.dma_start(
-                out=w2_sc_raw[32 * q : 32 * q + 4, :, :].bitcast(I32),
-                in_=w2_scales[:, 4 * q : 4 * q + 4, :].rearrange("a r c -> r a c").bitcast(I32),
-            )
-
-        def load_tab_scales(n):
-            a, q = divmod(n, QUADS)
-            nc.sync.dma_start(
-                out=tab_sc[32 * q + 4 * a : 32 * q + 4 * a + 4, :].bitcast(I32),
-                in_=tab_scales[a, 4 * q : 4 * q + 4, :].bitcast(I32),
-            )
+        nc.gpsimd.memset(tab_sc[:].bitcast(I32), 0)
+        nc.vector.memset(w2_sc_raw[:].rearrange("p a c -> p (a c)").bitcast(I32), 0)
 
         def load_w1(a, c0, width, tag, bufs):
             raw = keep.tile([P, PACK, width], F32, name=f"w1_raw{a}_{c0}", tag=tag, bufs=bufs, align_bytes=64)
@@ -72,34 +60,45 @@ def tile_list_barrier_slot_scores_kernel(
             nc.sync.dma_start(out=words[:], in_=tab_words[a].rearrange("p t i -> p (t i)").bitcast(I32))
             return words
 
-        gain_sb = keep.tile([P, PASSES, PACK], F32, name="gain_sb")
-        w1_raw = {}
-        w1_raw[0, 0] = [load_w1(0, 0, PASS, "w1_raw", 3)]
-        w1_raw[1, 0] = [load_w1(1, 0, PASS, "w1_raw", 3)]
-        for n in range(5):
-            load_tab_scales(n)
-        tab_w = [load_tab(0)]
-        for n in range(5, 8):
-            load_tab_scales(n)
-        nc.sync.dma_start(idx1[:], offs)
-        tab_w.append(load_tab(1))
-        nc.sync.dma_start(out=gain_sb[:], in_=gain.rearrange("(b p t) -> p b t", b=PASSES, t=PACK))
-        w1_raw[0, 1] = [load_w1(0, PASS, PASS, "w1_raw", 3)]
-        w1_raw[1, 1] = [load_w1(1, PASS + PASS // 2 * n, PASS // 2, "w1_last", 2) for n in range(2)]
-
         w2_raw = [keep.tile([P, PASSES, H], U8, name=f"w2_raw{b}", align_bytes=64) for b in range(PASSES)]
-        wgs_sb = keep.tile([P, PACK, S], F32, name="wgs_sb")
-        wgs_rows = wgs.rearrange("(q t) j -> q t j", t=PACK)
-        page = [keep.tile([P, T2], F32, name=f"page{k}", tag=f"page{k}") for k in range(SLICES)]
-        lim_sb = [keep.tile([P, J], F32, name=f"lim{k}") for k in range(SLICES)]
-        vec_sb = keep.tile([P, PASSES, PACK], F32, name="vec_sb")
-        slot_sb = keep.tile([P, T2 // P], F32, name="slot_sb")
 
         def load_w2(b):
             nc.sync.dma_start(
                 out=w2_raw[b][:].bitcast(I32),
                 in_=w2_words[:, :, H * b : H * (b + 1)].rearrange("a p c -> p a c").bitcast(I32),
             )
+
+        gain_sb = keep.tile([P, PASSES, PACK], F32, name="gain_sb")
+        w1_raw = {}
+        vec_sb = keep.tile([P, PASSES, PACK], F32, name="vec_sb")
+        tab_w = [load_tab(0)]
+        for q in range(QUADS):
+            nc.scalar.dma_start(
+                out=tab_sc[32 * q : 32 * q + 8, :].bitcast(I32),
+                in_=tab_scales[:, 4 * q : 4 * q + 4, :].bitcast(I32),
+            )
+        nc.sync.dma_start(idx1[:], offs)
+        w1_raw[0, 0] = [load_w1(0, PASS // 2 * n, PASS // 2, "w1_half", 8) for n in range(2)]
+        nc.sync.dma_start(idx2[:], offs2)
+        nc.sync.dma_start(idx3[:], offs3)
+        nc.sync.dma_start(out=gain_sb[:], in_=gain.rearrange("(b p t) -> p b t", b=PASSES, t=PACK))
+        nc.sync.dma_start(out=vec_sb[:], in_=vec.rearrange("(b p t) -> p b t", b=PASSES, t=PACK))
+        tab_w.append(load_tab(1))
+        for q in range(QUADS):
+            nc.sync.dma_start(
+                out=w2_sc_raw[32 * q : 32 * q + 4, :, :].bitcast(I32),
+                in_=w2_scales[:, 4 * q : 4 * q + 4, :].rearrange("a r c -> r a c").bitcast(I32),
+            )
+        load_w2(0)
+        w1_raw[1, 0] = [load_w1(1, PASS // 2 * n, PASS // 2, "w1_half", 8) for n in range(2)]
+        w1_raw[0, 1] = [load_w1(0, PASS + PASS // 2 * n, PASS // 2, "w1_half", 8) for n in range(2)]
+        w1_raw[1, 1] = [load_w1(1, PASS + PASS // 2 * n, PASS // 2, "w1_half", 8) for n in range(2)]
+
+        wgs_sb = keep.tile([P, PACK, S], F32, name="wgs_sb")
+        wgs_rows = wgs.rearrange("(q t) j -> q t j", t=PACK)
+        page = [keep.tile([P, T2], F32, name=f"page{k}", tag=f"page{k}") for k in range(SLICES)]
+        lim_sb = [keep.tile([P, J], F32, name=f"lim{k}") for k in range(SLICES)]
+        slot_sb = keep.tile([P, T2 // P], F32, name="slot_sb")
 
         def load_wgs(cols):
             for q in range(QUADS):
@@ -110,16 +109,12 @@ def tile_list_barrier_slot_scores_kernel(
             rows = src[PASS * b : PASS * (b + 1), :].rearrange("(p t) m -> p t m", t=PACK)
             nc.sync.dma_start(out=dst[k][:], in_=rows[:, t, :])
 
-        load_w2(0)
-        nc.sync.dma_start(idx2[:], offs2)
         load_wgs(halves[0])
         load_rows(page, page0, 0)
         load_rows(page, page0, 1)
         load_w2(1)
         load_wgs(halves[1])
         load_rows(page, page0, 2)
-        nc.sync.dma_start(idx3[:], offs3)
-        nc.sync.dma_start(out=vec_sb[:], in_=vec.rearrange("(b p t) -> p b t", b=PASSES, t=PACK))
         load_rows(lim_sb, lim, 0)
         load_rows(lim_sb, lim, 1)
         for k in range(3, SLICES):
@@ -130,13 +125,14 @@ def tile_list_barrier_slot_scores_kernel(
             nc.sync.dma_start(out=slot_sb[:], in_=slot.rearrange("(i p) -> p i", p=P))
 
         w2_codes = [keep.tile([P, PASSES, H], U8, name=f"w2_codes{b}", align_bytes=64) for b in range(PASSES)]
-        w2_sc = keep.tile([P, PASSES, H], U8, name="w2_sc", align_bytes=64)
-        nc.vector.tensor_copy(
-            out=w2_sc[:].rearrange("p a (b t q) -> p (a b) t q", t=PACK, q=P),
-            in_=w2_sc_raw[:].rearrange("p a (b q t) -> p (a b) t q", t=PACK, q=P),
-        )
+
+        w2_sc = [keep.tile([P, PASSES, PASS], U8, name=f"w2_sc{b}", align_bytes=64) for b in range(PASSES)]
 
         def deal_w2(b):
+            nc.vector.tensor_copy(
+                out=w2_sc[b][:].rearrange("p a (t q) -> p a t q", q=P),
+                in_=w2_sc_raw[:, :, PASS * b : PASS * (b + 1)].rearrange("p a (q t) -> p a t q", t=PACK),
+            )
             nc.vector.tensor_copy(
                 out=w2_codes[b][:].rearrange("p a c -> p (a c)").bitcast(U16).rearrange("p (a t q) -> p a t q", t=PACK, q=P),
                 in_=w2_raw[b][:].rearrange("p a c -> p (a c)").bitcast(U16).rearrange("p (a q t) -> p a t q", t=PACK, q=P),
@@ -151,7 +147,7 @@ def tile_list_barrier_slot_scores_kernel(
             share = P // len(w1_raw[a, b])
             for n, raw in enumerate(w1_raw[a, b]):
                 src = raw[:].rearrange("p j (m t) -> p m t j", t=PACK)
-                if on_scalar:
+                if n in on_scalar:
                     nc.scalar.copy(out=dst[:, share * n : share * (n + 1), :, :], in_=src)
                 else:
                     nc.vector.tensor_copy(out=dst[:, share * n : share * (n + 1), :, :], in_=src)
@@ -187,13 +183,13 @@ def tile_list_barrier_slot_scores_kernel(
         th = [keep.tile([P, PACK, S], F32, name=f"th{b}") for b in range(PASSES)]
         act_codes = [keep.tile([P, S], U32, name=f"act_codes{b}", align_bytes=64) for b in range(PASSES)]
         act_sc = [keep.tile([P, S], U8, name=f"act_sc{b}", align_bytes=64) for b in range(PASSES)]
-        planes = {
-            (b, u): keep.tile([P, PACK, HALF], BF16, name=f"act_planes{b}{u}", align_bytes=64)
-            for b in range(PASSES)
-            for u in range(2)
-        }
+        planes = {}
 
         def scale_act(b, t, u):
+            if (b, u) not in planes:
+                planes[b, u] = keep.tile(
+                    [P, PACK, HALF], BF16, name=f"act_planes{b}{u}", tag=f"act_woven{b}0", align_bytes=64
+                )
             nc.scalar.activation(
                 out=planes[b, u][:, t, :], in_=th[b][:, t, halves[u]], func=ACT.Copy, scale=gain_sb[:, b, t : t + 1]
             )
@@ -219,44 +215,61 @@ def tile_list_barrier_slot_scores_kernel(
                 in_=woven_act[b, u][:].rearrange("p j t -> p (j t)"),
             )
 
-        everything = slice(0, S)
-        prepare_w1(0, 0, True, 1)
-        prepare_w1(1, 0, True, 1)
-        nc.vector.tensor_copy(v_sc[:], tab_sc[:].indirect(idx1[:]))
-        y_low = [bank(PACK + t) for t in range(PACK)]
-        for a in range(PASSES):
-            nc.vector.tensor_copy(v_w[a][:], tab_w[a][:].bitcast(U32).indirect(idx1[:]))
+        def scale_and_weave_act(b, u):
+            woven_act[b, u] = keep.tile(
+                [P, HALF, PACK], BF16, name=f"act_woven{b}{u}", tag=f"act_woven{b}{u}", align_bytes=64
+            )
+            nc.vector.tensor_tensor(
+                woven_act[b, u][:].rearrange("p (c i) t -> p c t i", i=4),
+                th[b][:, :, halves[u]].rearrange("p t (c i) -> p c t i", i=4),
+                gain_sb[:, b, :].unsqueeze(1).unsqueeze(3).to_broadcast([P, HALF // 4, PACK, 4]),
+                ALU.mult,
+            )
+
+        y1 = {}
+
+        def stage1_pass(a, b, u):
             for t in range(PACK):
-                stage1(y_low[t][:], a, 0, t, everything, a == 0, a == PASSES - 1)
-        for t in range(PACK):
-            nc.scalar.activation(out=th[0][:, t, :], in_=y_low[t][:], func=ACT.Tanh)
-            scale_act(0, t, 0)
-        y_high = [bank(n) for n in range(PACK)]
-        for a in range(PASSES):
-            prepare_w1(a, 1, False, 1 + a)
-            for u in range(2):
-                for t in range(PACK):
-                    dst = y_high[2 * u + t // 2][:, HALF * (t % 2) : HALF * (t % 2 + 1)]
-                    stage1(dst, a, 1, t, halves[u], a == 0 and t % 2 == 0, a == PASSES - 1 and t % 2 == 1)
-        weave_act(0, 0, "vector")
-        quant_act(0, 0)
-        deal_w2(0)
-        for u in range(2):
+                pair = t // 2
+                if (b, u, pair) not in y1:
+                    y1[b, u, pair] = bank(PACK * (1 - b) + 2 * u + pair)
+                dst = y1[b, u, pair][:, HALF * (t % 2) : HALF * (t % 2 + 1)]
+                stage1(dst, a, b, t, halves[u], a == 0 and t % 2 == 0, a == PASSES - 1 and t % 2 == 1)
+
+        def features(b, u):
             for pair in range(2):
                 nc.scalar.activation(
-                    out=th[1][:, 2 * pair : 2 * pair + 2, halves[u]],
-                    in_=y_high[2 * u + pair][:].rearrange("p (t j) -> p t j", t=2),
+                    out=th[b][:, 2 * pair : 2 * pair + 2, halves[u]],
+                    in_=y1[b, u, pair][:].rearrange("p (t j) -> p t j", t=2),
                     func=ACT.Tanh,
                 )
-                for t in range(2 * pair, 2 * pair + 2):
-                    scale_act(1, t, u)
-            if u == 0:
-                weave_act(1, 0, "vector")
-                quant_act(1, 0)
-        weave_act(1, 1, "scalar")
-        for t in range(PACK):
-            scale_act(0, t, 1)
-        weave_act(0, 1, "scalar")
+
+        everything = slice(0, S)
+        nc.vector.tensor_copy(v_sc[:], tab_sc[:].indirect(idx1[:]))
+        for a in range(PASSES):
+            nc.vector.tensor_copy(v_w[a][:], tab_w[a][:].bitcast(U32).indirect(idx1[:]))
+            prepare_w1(a, 0, [0, 1], 1)
+            for u in range(2):
+                stage1_pass(a, 0, u)
+        deal_w2(0)
+        prepare_w1(0, 1, [1], 1)
+        features(0, 0)
+        for u in range(2):
+            stage1_pass(0, 1, u)
+        prepare_w1(1, 1, [], 2)
+        for u in range(2):
+            stage1_pass(1, 1, u)
+        scale_and_weave_act(0, 0)
+        quant_act(0, 0)
+        features(1, 0)
+        scale_and_weave_act(1, 0)
+        quant_act(1, 0)
+        for b in range(PASSES):
+            features(b, 1)
+        for b in range(PASSES):
+            for t in range(PACK):
+                scale_act(b, t, 1)
+            weave_act(b, 1, "scalar")
 
         y2 = {}
 
@@ -271,7 +284,7 @@ def tile_list_barrier_slot_scores_kernel(
                     nc.tensor.matmul_mx(
                         out=y2[k][:, c0 : c0 + width],
                         lhsT=w2_codes[b][:, a, 2 * P * t : 2 * P * (t + 1)].bitcast(FP4X4),
-                        lhsT_scale=w2_sc[:, a, P * k : P * (k + 1)],
+                        lhsT_scale=w2_sc[b][:, a, P * t : P * (t + 1)],
                         rhs=act_codes[a][:, c0 : c0 + width].bitcast(FP8X4),
                         rhs_scale=act_sc[a][:, c0 : c0 + width],
                         start=(a == 0 and c0 == starts[0]),
@@ -366,8 +379,8 @@ def tile_list_barrier_slot_scores_kernel(
         put(0, halves[0])
         meet(2, halves[0])
         put(1, halves[0])
-        quant_act(1, 1)
         quant_act(0, 1)
+        quant_act(1, 1)
         deal_w2(1)
         for k in range(early):
             stage2(k, halves[1])

from contextlib import ExitStack

import concourse.mybir as mybir

K, H, T, S, T2, J = 1024, 1024, 2048, 512, 1024, 512
FLOPS = 2 * K * H * S + 2 * H * H * S + 2 * H * T2 * J

F32 = mybir.dt.float32
BF16 = mybir.dt.bfloat16
I32 = mybir.dt.int32
U32 = mybir.dt.uint32
U16 = mybir.dt.uint16
U8 = mybir.dt.uint8
FP8X4 = mybir.dt.float8_e4m3fn_x4
FP4X4 = mybir.dt.float4_e2m1fn_x4
ALU = mybir.AluOpType
ACT = mybir.ActivationFunctionType

P = 128
PACK = 4
PASS = P * PACK
PASSES = 2
SLICES = PASSES * PACK
QUADS = 4


def tile_list_barrier_slot_scores_kernel(
    tc, tab_words, tab_scales, offs, w1, gain, w2_words, w2_scales, wgs, page0, offs2, offs3, lim, vec, slot, out
):
    nc = tc.nc
    with ExitStack() as ctx:
        lists = ctx.enter_context(tc.tile_pool(name="lists", bufs=1))
        keep = ctx.enter_context(tc.tile_pool(name="keep", bufs=1))
        ring = ctx.enter_context(tc.tile_pool(name="ring", bufs=2))
        psum = ctx.enter_context(tc.psum_pool(name="psum", bufs=1))

        idx1 = lists.tile([P, S // 16], U16, name="idx1")
        idx2 = lists.tile([P, S // 16], U16, name="idx2")
        idx3 = lists.tile([P, J // 16], U16, name="idx3")

        def bank(k):
            return psum.tile([P, 512], F32, name=f"bank{k}", tag=f"bank{k}")

        HALF = S // 2
        halves = [slice(0, HALF), slice(HALF, S)]
        tab_sc = keep.tile([P, T], U8, name="tab_sc", align_bytes=64)
        w2_sc_raw = keep.tile([P, PASSES, H], U8, name="w2_sc_raw", align_bytes=64)
        nc.gpsimd.memset(tab_sc[:].bitcast(I32), 0)
        nc.vector.memset(w2_sc_raw[:].rearrange("p a c -> p (a c)").bitcast(I32), 0)

        def load_w1(a, c0, width, tag, bufs):
            raw = keep.tile([P, PACK, width], F32, name=f"w1_raw{a}_{c0}", tag=tag, bufs=bufs, align_bytes=64)
            nc.sync.dma_start(
                out=raw[:], in_=w1[PASS * a : PASS * (a + 1), c0 : c0 + width].rearrange("(p j) c -> p j c", j=PACK)
            )
            return raw

        def load_tab(a):
            words = keep.tile([P, T], I32, name=f"tab_w{a}", tag="wide", bufs=2, align_bytes=64)
            nc.sync.dma_start(out=words[:], in_=tab_words[a].rearrange("p t i -> p (t i)").bitcast(I32))
            return words

        w2_raw = [keep.tile([P, PASSES, H], U8, name=f"w2_raw{b}", align_bytes=64) for b in range(PASSES)]

        def load_w2(b):
            nc.sync.dma_start(
                out=w2_raw[b][:].bitcast(I32),
                in_=w2_words[:, :, H * b : H * (b + 1)].rearrange("a p c -> p a c").bitcast(I32),
            )

        gain_sb = keep.tile([P, PASSES, PACK], F32, name="gain_sb")
        w1_raw = {}
        vec_sb = keep.tile([P, PASSES, PACK], F32, name="vec_sb")
        tab_w = [load_tab(0)]
        for q in range(QUADS):
            nc.scalar.dma_start(
                out=tab_sc[32 * q : 32 * q + 8, :].bitcast(I32),
                in_=tab_scales[:, 4 * q : 4 * q + 4, :].bitcast(I32),
            )
        nc.sync.dma_start(idx1[:], offs)
        w1_raw[0, 0] = [load_w1(0, PASS // 2 * n, PASS // 2, "w1_half", 8) for n in range(2)]
        nc.sync.dma_start(idx2[:], offs2)
        nc.sync.dma_start(idx3[:], offs3)
        nc.sync.dma_start(out=gain_sb[:], in_=gain.rearrange("(b p t) -> p b t", b=PASSES, t=PACK))
        nc.sync.dma_start(out=vec_sb[:], in_=vec.rearrange("(b p t) -> p b t", b=PASSES, t=PACK))
        tab_w.append(load_tab(1))
        for q in range(QUADS):
            nc.sync.dma_start(
                out=w2_sc_raw[32 * q : 32 * q + 4, :, :].bitcast(I32),
                in_=w2_scales[:, 4 * q : 4 * q + 4, :].rearrange("a r c -> r a c").bitcast(I32),
            )
        load_w2(0)
        w1_raw[1, 0] = [load_w1(1, PASS // 2 * n, PASS // 2, "w1_half", 8) for n in range(2)]
        w1_raw[0, 1] = [load_w1(0, PASS + PASS // 2 * n, PASS // 2, "w1_half", 8) for n in range(2)]
        w1_raw[1, 1] = [load_w1(1, PASS + PASS // 2 * n, PASS // 2, "w1_half", 8) for n in range(2)]

        wgs_sb = keep.tile([P, PACK, S], F32, name="wgs_sb")
        wgs_rows = wgs.rearrange("(q t) j -> q t j", t=PACK)
        page = [keep.tile([P, T2], F32, name=f"page{k}", tag=f"page{k}") for k in range(SLICES)]
        lim_sb = [keep.tile([P, J], F32, name=f"lim{k}") for k in range(SLICES)]
        slot_sb = keep.tile([P, T2 // P], F32, name="slot_sb")

        def load_wgs(cols):
            for q in range(QUADS):
                nc.sync.dma_start(out=wgs_sb[32 * q : 32 * (q + 1), :, cols], in_=wgs_rows[:, :, cols])

        def load_rows(dst, src, k):
            b, t = divmod(k, PACK)
            rows = src[PASS * b : PASS * (b + 1), :].rearrange("(p t) m -> p t m", t=PACK)
            nc.sync.dma_start(out=dst[k][:], in_=rows[:, t, :])

        load_wgs(halves[0])
        load_rows(page, page0, 0)
        load_rows(page, page0, 1)
        load_w2(1)
        load_wgs(halves[1])
        load_rows(page, page0, 2)
        load_rows(lim_sb, lim, 0)
        load_rows(lim_sb, lim, 1)
        for k in range(3, SLICES):
            load_rows(page, page0, k)
            load_rows(lim_sb, lim, k - 1)
        load_rows(lim_sb, lim, SLICES - 1)
        with nc.allow_non_contiguous_dma(reason="one float32 for each partition and output tile"):
            nc.sync.dma_start(out=slot_sb[:], in_=slot.rearrange("(i p) -> p i", p=P))

        w2_codes = [keep.tile([P, PASSES, H], U8, name=f"w2_codes{b}", align_bytes=64) for b in range(PASSES)]

        w2_sc = [keep.tile([P, PASSES, PASS], U8, name=f"w2_sc{b}", align_bytes=64) for b in range(PASSES)]

        def deal_w2(b):
            nc.vector.tensor_copy(
                out=w2_sc[b][:].rearrange("p a (t q) -> p a t q", q=P),
                in_=w2_sc_raw[:, :, PASS * b : PASS * (b + 1)].rearrange("p a (q t) -> p a t q", t=PACK),
            )
            nc.vector.tensor_copy(
                out=w2_codes[b][:].rearrange("p a c -> p (a c)").bitcast(U16).rearrange("p (a t q) -> p a t q", t=PACK, q=P),
                in_=w2_raw[b][:].rearrange("p a c -> p (a c)").bitcast(U16).rearrange("p (a q t) -> p a t q", t=PACK, q=P),
            )

        w1_codes = {}
        w1_sc = {}

        def prepare_w1(a, b, on_scalar, quant_parts):
            grouped = ring.tile([P, PACK, P, PACK], BF16, name="w1_bf", align_bytes=64)
            dst = grouped[:].rearrange("p t m j -> p m t j")
            share = P // len(w1_raw[a, b])
            for n, raw in enumerate(w1_raw[a, b]):
                src = raw[:].rearrange("p j (m t) -> p m t j", t=PACK)
                if n in on_scalar:
                    nc.scalar.copy(out=dst[:, share * n : share * (n + 1), :, :], in_=src)
                else:
                    nc.vector.tensor_copy(out=dst[:, share * n : share * (n + 1), :, :], in_=src)
            codes = keep.tile([P, PASS], U32, name=f"w1_codes{a}{b}", align_bytes=64)
            scales = keep.tile([P, PASS], U8, name=f"w1_sc{a}{b}", align_bytes=64)
            flat = grouped[:].rearrange("p t m j -> p (t m j)")
            width = PASS // quant_parts
            for n in range(quant_parts):
                cols = slice(width * n, width * (n + 1))
                nc.vector.quantize_mx(
                    out=codes[:, cols].bitcast(FP8X4),
                    scales=scales[:, cols],
                    in_=flat[:, PACK * width * n : PACK * width * (n + 1)],
                )
            w1_codes[a, b] = codes
            w1_sc[a, b] = scales

        v_sc = keep.tile([P, S], U8, name="v_sc", align_bytes=64)
        v_w = [keep.tile([P, S], U32, name=f"v_w{a}", align_bytes=64) for a in range(PASSES)]

        def stage1(dst, a, b, t, cols, start, stop):
            m_cols = slice(P * t, P * (t + 1))
            nc.tensor.matmul_mx(
                out=dst,
                lhsT=w1_codes[a, b][:, m_cols].bitcast(FP8X4),
                lhsT_scale=w1_sc[a, b][:, m_cols],
                rhs=v_w[a][:, cols].bitcast(FP8X4),
                rhs_scale=v_sc[4 * a : P, cols],
                start=start,
                stop=stop,
            )

        th = [keep.tile([P, PACK, S], F32, name=f"th{b}") for b in range(PASSES)]
        act_codes = [keep.tile([P, S], U32, name=f"act_codes{b}", align_bytes=64) for b in range(PASSES)]
        act_sc = [keep.tile([P, S], U8, name=f"act_sc{b}", align_bytes=64) for b in range(PASSES)]
        planes = {}

        def scale_act(b, t, u):
            if (b, u) not in planes:
                planes[b, u] = keep.tile(
                    [P, PACK, HALF], BF16, name=f"act_planes{b}{u}", tag=f"act_woven{b}0", align_bytes=64
                )
            nc.scalar.activation(
                out=planes[b, u][:, t, :], in_=th[b][:, t, halves[u]], func=ACT.Copy, scale=gain_sb[:, b, t : t + 1]
            )

        def weave(engine, woven, src):
            dst_view = woven.rearrange("p (c i) t -> p c t i", i=4)
            src_view = src.rearrange("p t (c i) -> p c t i", i=4)
            if engine == "scalar":
                nc.scalar.copy(out=dst_view, in_=src_view)
            else:
                nc.vector.tensor_copy(out=dst_view, in_=src_view)

        woven_act = {}

        def weave_act(b, u, engine):
            woven_act[b, u] = keep.tile([P, HALF, PACK], BF16, name=f"act_woven{b}{u}", align_bytes=64)
            weave(engine, woven_act[b, u][:], planes[b, u][:])

        def quant_act(b, u):
            nc.vector.quantize_mx(
                out=act_codes[b][:, halves[u]].bitcast(FP8X4),
                scales=act_sc[b][:, halves[u]],
                in_=woven_act[b, u][:].rearrange("p j t -> p (j t)"),
            )

        def scale_and_weave_act(b, u):
            woven_act[b, u] = keep.tile(
                [P, HALF, PACK], BF16, name=f"act_woven{b}{u}", tag=f"act_woven{b}{u}", align_bytes=64
            )
            nc.vector.tensor_tensor(
                woven_act[b, u][:].rearrange("p (c i) t -> p c t i", i=4),
                th[b][:, :, halves[u]].rearrange("p t (c i) -> p c t i", i=4),
                gain_sb[:, b, :].unsqueeze(1).unsqueeze(3).to_broadcast([P, HALF // 4, PACK, 4]),
                ALU.mult,
            )

        y1 = {}

        def stage1_pass(a, b, u):
            for t in range(PACK):
                pair = t // 2
                if (b, u, pair) not in y1:
                    y1[b, u, pair] = bank(PACK * (1 - b) + 2 * u + pair)
                dst = y1[b, u, pair][:, HALF * (t % 2) : HALF * (t % 2 + 1)]
                stage1(dst, a, b, t, halves[u], a == 0 and t % 2 == 0, a == PASSES - 1 and t % 2 == 1)

        def features(b, u):
            for pair in range(2):
                nc.scalar.activation(
                    out=th[b][:, 2 * pair : 2 * pair + 2, halves[u]],
                    in_=y1[b, u, pair][:].rearrange("p (t j) -> p t j", t=2),
                    func=ACT.Tanh,
                )

        everything = slice(0, S)
        nc.vector.tensor_copy(v_sc[:], tab_sc[:].indirect(idx1[:]))
        for a in range(PASSES):
            nc.vector.tensor_copy(v_w[a][:], tab_w[a][:].bitcast(U32).indirect(idx1[:]))
            prepare_w1(a, 0, [0, 1], 1)
            for u in range(2):
                stage1_pass(a, 0, u)
        deal_w2(0)
        prepare_w1(0, 1, [1], 1)
        features(0, 0)
        for u in range(2):
            stage1_pass(0, 1, u)
        prepare_w1(1, 1, [], 2)
        for u in range(2):
            stage1_pass(1, 1, u)
        scale_and_weave_act(0, 0)
        quant_act(0, 0)
        features(1, 0)
        scale_and_weave_act(1, 0)
        quant_act(1, 0)
        for b in range(PASSES):
            features(b, 1)
        for b in range(PASSES):
            for t in range(PACK):
                scale_act(b, t, 1)
            weave_act(b, 1, "scalar")

        y2 = {}

        def stage2(k, cols):
            b, t = divmod(k, PACK)
            if k not in y2:
                y2[k] = bank((k + PACK) % SLICES)
            width = S if cols == everything else P
            starts = list(range(cols.start, cols.stop, width))
            for a in range(PASSES):
                for c0 in starts:
                    nc.tensor.matmul_mx(
                        out=y2[k][:, c0 : c0 + width],
                        lhsT=w2_codes[b][:, a, 2 * P * t : 2 * P * (t + 1)].bitcast(FP4X4),
                        lhsT_scale=w2_sc[b][:, a, P * t : P * (t + 1)],
                        rhs=act_codes[a][:, c0 : c0 + width].bitcast(FP8X4),
                        rhs_scale=act_sc[a][:, c0 : c0 + width],
                        start=(a == 0 and c0 == starts[0]),
                        stop=(a == PASSES - 1 and c0 == starts[-1]),
                    )

        page_planes = keep.tile([P, PACK, T2], BF16, name="page_planes", align_bytes=64)
        x_planes = keep.tile([P, PACK, J], BF16, name="x_planes", align_bytes=64)
        page_bf = [
            keep.tile([P, T2, PACK], BF16, name=f"page_bf{b}", tag="wide", bufs=2, align_bytes=64) for b in range(PASSES)
        ]
        x_bf = [keep.tile([P, J, PACK], BF16, name=f"x_bf{b}", tag=f"x_bf{b}", align_bytes=64) for b in range(PASSES)]
        page_codes = [keep.tile([P, T2], U32, name=f"page_codes{b}", align_bytes=64) for b in range(PASSES)]
        page_sc = [keep.tile([P, T2], U8, name=f"page_sc{b}", align_bytes=64) for b in range(PASSES)]
        x_codes = [keep.tile([P, J], U32, name=f"x_codes{b}", align_bytes=64) for b in range(PASSES)]
        x_sc = [keep.tile([P, J], U8, name=f"x_sc{b}", align_bytes=64) for b in range(PASSES)]
        e = {}
        h = {}
        picked = {}
        top = {}
        last = SLICES - 1

        def meet(k, cols, dst=None):
            b, t = divmod(k, PACK)
            if dst is None:
                fresh = ring.tile([P, S], F32, name="h", bufs=3)
                dst = fresh[:]
            h[k, cols.start] = dst[:, cols]
            nc.vector.scalar_tensor_tensor(
                dst[:, cols], th[b][:, t, cols], gain_sb[:, b, t : t + 1], y2[k][:, cols], ALU.mult, ALU.max
            )

        def put(k, cols):
            places = idx2[:, cols.start // 16 : cols.stop // 16]
            nc.vector.tensor_tensor(page[k][:].indirect(places), h[k, cols.start], wgs_sb[:, k % PACK, cols], ALU.mult)

        def round_page(k, cols):
            b, t = divmod(k, PACK)
            dst = page_planes[:, t, cols] if b == 0 else page_bf[b][:, cols, t]
            nc.scalar.copy(out=dst, in_=page[k][:, cols])

        def pick(k, dst=None):
            if dst is None:
                fresh = ring.tile([P, J], F32, name="picked")
                dst = fresh[:]
            picked[k] = dst
            nc.vector.tensor_copy(dst, page[k][:].indirect(idx3[:]))

        def limit(k):
            b, t = divmod(k, PACK)
            top[k] = top[k - 1] if k == last else ring.tile([P, J], F32, name="top", bufs=4)
            nc.vector.tensor_tensor(top[k][:], picked[k], lim_sb[k][:], ALU.max)
            factor = vec_sb[:, b, t : t + 1]
            if k == last:
                nc.vector.tensor_scalar(x_bf[b][:, :, t], top[k][:], factor, None, ALU.mult)
            else:
                dst = x_planes[:, t, :] if b == 0 else x_bf[b][:, :, t]
                nc.scalar.activation(out=dst, in_=top[k][:], func=ACT.Copy, scale=factor)

        def quant_page(b, cols):
            nc.vector.quantize_mx(
                out=page_codes[b][:, cols].bitcast(FP8X4),
                scales=page_sc[b][:, cols],
                in_=page_bf[b][:, cols, :].rearrange("p m t -> p (m t)"),
            )

        def quant_x(b):
            nc.vector.quantize_mx(
                out=x_codes[b][:].bitcast(FP8X4), scales=x_sc[b][:], in_=x_bf[b][:].rearrange("p j t -> p (j t)")
            )

        def stage3(i, b):
            if b == 0:
                e[i] = bank((i + PACK) % SLICES)
            cols = slice(P * i, P * (i + 1))
            nc.tensor.matmul_mx(
                out=e[i][:],
                lhsT=page_codes[b][:, cols].bitcast(FP8X4),
                lhsT_scale=page_sc[b][:, cols],
                rhs=x_codes[b][:].bitcast(FP8X4),
                rhs_scale=x_sc[b][:],
                start=(b == 0),
                stop=(b == PASSES - 1),
            )

        whole = slice(0, T2)
        early = 3
        for k in range(early):
            stage2(k, halves[0])
        meet(0, halves[0])
        meet(1, halves[0])
        put(0, halves[0])
        meet(2, halves[0])
        put(1, halves[0])
        quant_act(0, 1)
        quant_act(1, 1)
        deal_w2(1)
        for k in range(early):
            stage2(k, halves[1])
        for k in range(early, SLICES):
            stage2(k, everything)
        put(2, halves[0])
        units = [(k, halves[1] if k < early else everything) for k in range(SLICES)]
        meet(*units[0])
        for k in range(last):
            if k + 1 < last:
                meet(*units[k + 1])
            if k > 0:
                pick(k - 1)
            put(*units[k])
            round_page(k, whole)
            if k == PACK - 1:
                weave("scalar", page_bf[0][:], page_planes[:])
            if k > 0:
                limit(k - 1)
            if k == PACK:
                weave("scalar", x_bf[0][:], x_planes[:])
        quant_page(0, whole)
        quant_x(0)
        late = keep.tile([P, 2, S], F32, name="late", tag="x_bf0", align_bytes=64)
        for i in range(last):
            stage3(i, 0)
        pick(last - 1, late[:, 0, :])
        meet(last, everything, late[:, 1, :])
        stage3(last, 0)
        limit(last - 1)
        put(last, everything)
        chunk = 256
        for c in range(T2 // chunk):
            round_page(last, slice(chunk * c, chunk * (c + 1)))
        pick(last)
        quant_page(1, slice(0, chunk))
        limit(last)
        quant_page(1, slice(chunk, 2 * chunk))
        quant_x(1)
        for c in range(T2 // chunk):
            if c >= 2:
                quant_page(1, slice(chunk * c, chunk * (c + 1)))
            for i in range(2 * c, 2 * c + 2):
                stage3(i, 1)

        for i in range(T2 // P):
            staged = keep.tile([P, 2, J], F32, name=f"staged{i}", tag=f"page{i}")
            nc.scalar.activation(out=staged[:, 0, :], in_=e[i][:], func=ACT.Abs)
            nc.vector.tensor_scalar(staged[:, 1, :], staged[:, 0, :], slot_sb[:, i : i + 1], None, ALU.min)
            nc.sync.dma_start(out=out[P * i : P * (i + 1), :], in_=staged[:, 1, :])
